import numpy as np
import ml_dtypes

BF16 = ml_dtypes.bfloat16


def bf(x):
    return np.asarray(x, np.float32).astype(BF16)


def f32(x):
    return np.asarray(x, np.float32)


def f64(x):
    return np.asarray(x).astype(np.float64)


def striped(idx):
    return np.concatenate([l.reshape(-1, 16).T for l in idx])


def rows(idx, k):
    return np.tile(np.repeat(idx, 16, axis=0), (k // (16 * 8), 1))


def look(tab, idx):
    return np.take_along_axis(f64(tab), rows(idx, len(tab)), axis=1)


K, S, V, N = 128, 2048, 2048, 2048


def setup_inputs():
    return {"tab": f32(np.random.standard_normal((2, K, S))), "y": f32(1.0 * np.random.standard_normal((K, V))), "offs": striped(np.stack([np.random.permutation(S)[:N] for _ in range(8)]))}


def reference(tab, y, offs):
    idx = np.stack([g.T.reshape(-1) for g in np.split(offs, 8)])
    x = np.maximum(look(tab[0], idx), f64(y)) * np.tanh(look(tab[1], idx))
    return x

@@ -1,0 +1,35 @@
+import concourse.mybir as mybir
+
+F32, U16 = mybir.dt.float32, mybir.dt.uint16
+MAX, MULT = mybir.AluOpType.max, mybir.AluOpType.mult
+TANH = mybir.ActivationFunctionType.Tanh
+
+ROWS, PLACES, COLUMNS = 128, 2048, 2048
+PIECE = 512
+OFFSETS = PIECE // 16
+PIECES = COLUMNS // PIECE
+
+
+def tile_lookup_maxgate_out_kernel(tc, tab, y, offs, out):
+    nc = tc.nc
+    with tc.tile_pool(name="held", bufs=1) as held:
+        offsets = held.tile([ROWS, COLUMNS // 16], U16, name="offsets")
+        floors = held.tile([ROWS, PLACES], F32, name="floors")
+        gates = held.tile([ROWS, PLACES], F32, name="gates")
+        stream = held.tile([ROWS, COLUMNS], F32, name="stream")
+        nc.sync.dma_start(offsets[:], offs)
+        nc.sync.dma_start(floors[:], tab[0])
+        nc.sync.dma_start(stream[:], y)
+        nc.sync.dma_start(gates[:], tab[1])
+        raised = [held.tile([ROWS, PIECE], F32, name=f"raised{p}") for p in range(PIECES)]
+        gate = [held.tile([ROWS, PIECE], F32, name=f"gate{p}") for p in range(PIECES)]
+        result = [held.tile([ROWS, PIECE], F32, name=f"result{p}") for p in range(PIECES)]
+        for p in range(PIECES):
+            entries = offsets[:, p * OFFSETS : (p + 1) * OFFSETS]
+            columns = slice(p * PIECE, (p + 1) * PIECE)
+            nc.vector.tensor_tensor(raised[p][:], floors[:].indirect(entries), stream[:, columns], MAX)
+            nc.scalar.activation(gate[p][:], gates[:].indirect(entries), TANH)
+        for p in range(PIECES):
+            columns = slice(p * PIECE, (p + 1) * PIECE)
+            nc.vector.tensor_tensor(result[p][:], raised[p][:], gate[p][:], MULT)
+            nc.sync.dma_start(out[:, columns], result[p][:])

@@ -21,6 +21,11 @@ def tile_lookup_maxgate_out_kernel(tc, tab, y, offs, out):
         nc.sync.dma_start(floors[:], tab[0])
         nc.sync.dma_start(stream[:], y)
         nc.sync.dma_start(gates[:], tab[1])
+        zeros = held.tile([ROWS, 1], F32, name="zeros")
+        warm = held.tile([ROWS, 1], F32, name="warm")
+        nc.vector.memset(zeros[:], 0.0)
+        nc.scalar.activation(warm[:], zeros[:], TANH)
+
         raised = [held.tile([ROWS, PIECE], F32, name=f"raised{p}") for p in range(PIECES)]
         gate = [held.tile([ROWS, PIECE], F32, name=f"gate{p}") for p in range(PIECES)]
         result = [held.tile([ROWS, PIECE], F32, name=f"result{p}") for p in range(PIECES)]

@@ -16,25 +16,27 @@ def tile_lookup_maxgate_out_kernel(tc, tab, y, offs, out):
         offsets = held.tile([ROWS, COLUMNS // 16], U16, name="offsets")
         floors = held.tile([ROWS, PLACES], F32, name="floors")
         gates = held.tile([ROWS, PLACES], F32, name="gates")
-        stream = held.tile([ROWS, COLUMNS], F32, name="stream")
+        stream = [held.tile([ROWS, PIECE], F32, name=f"stream{p}") for p in range(PIECES)]
         nc.sync.dma_start(offsets[:], offs)
         nc.sync.dma_start(floors[:], tab[0])
-        nc.sync.dma_start(stream[:], y)
+        for p in range(1):
+            nc.sync.dma_start(stream[p][:], y[:, p * PIECE : (p + 1) * PIECE])
         nc.sync.dma_start(gates[:], tab[1])
+        for p in range(1, PIECES):
+            nc.sync.dma_start(stream[p][:], y[:, p * PIECE : (p + 1) * PIECE])
+        raised = [held.tile([ROWS, PIECE], F32, name=f"raised{p}") for p in range(PIECES)]
+        gate = [held.tile([ROWS, PIECE], F32, name=f"gate{p}") for p in range(PIECES)]
+        result = [held.tile([ROWS, PIECE], F32, name=f"result{p}") for p in range(PIECES)]
+
         zeros = held.tile([ROWS, 1], F32, name="zeros")
         warm = held.tile([ROWS, 1], F32, name="warm")
         nc.vector.memset(zeros[:], 0.0)
         nc.scalar.activation(warm[:], zeros[:], TANH)
 
-        raised = [held.tile([ROWS, PIECE], F32, name=f"raised{p}") for p in range(PIECES)]
-        gate = [held.tile([ROWS, PIECE], F32, name=f"gate{p}") for p in range(PIECES)]
-        result = [held.tile([ROWS, PIECE], F32, name=f"result{p}") for p in range(PIECES)]
         for p in range(PIECES):
             entries = offsets[:, p * OFFSETS : (p + 1) * OFFSETS]
-            columns = slice(p * PIECE, (p + 1) * PIECE)
-            nc.vector.tensor_tensor(raised[p][:], floors[:].indirect(entries), stream[:, columns], MAX)
+            nc.vector.tensor_tensor(raised[p][:], floors[:].indirect(entries), stream[p][:], MAX)
             nc.scalar.activation(gate[p][:], gates[:].indirect(entries), TANH)
         for p in range(PIECES):
-            columns = slice(p * PIECE, (p + 1) * PIECE)
             nc.vector.tensor_tensor(result[p][:], raised[p][:], gate[p][:], MULT)
-            nc.sync.dma_start(out[:, columns], result[p][:])
+            nc.sync.dma_start(out[:, p * PIECE : (p + 1) * PIECE], result[p][:])

import concourse.mybir as mybir

F32, U16 = mybir.dt.float32, mybir.dt.uint16
MAX, MULT = mybir.AluOpType.max, mybir.AluOpType.mult
TANH = mybir.ActivationFunctionType.Tanh

ROWS, PLACES, COLUMNS = 128, 2048, 2048
PIECE = 512
OFFSETS = PIECE // 16
PIECES = COLUMNS // PIECE


def tile_lookup_maxgate_out_kernel(tc, tab, y, offs, out):
    nc = tc.nc
    with tc.tile_pool(name="held", bufs=1) as held:
        offsets = held.tile([ROWS, COLUMNS // 16], U16, name="offsets")
        floors = held.tile([ROWS, PLACES], F32, name="floors")
        gates = held.tile([ROWS, PLACES], F32, name="gates")
        stream = [held.tile([ROWS, PIECE], F32, name=f"stream{p}") for p in range(PIECES)]
        nc.sync.dma_start(offsets[:], offs)
        nc.sync.dma_start(floors[:], tab[0])
        for p in range(1):
            nc.sync.dma_start(stream[p][:], y[:, p * PIECE : (p + 1) * PIECE])
        nc.sync.dma_start(gates[:], tab[1])
        for p in range(1, PIECES):
            nc.sync.dma_start(stream[p][:], y[:, p * PIECE : (p + 1) * PIECE])
        raised = [held.tile([ROWS, PIECE], F32, name=f"raised{p}") for p in range(PIECES)]
        gate = [held.tile([ROWS, PIECE], F32, name=f"gate{p}") for p in range(PIECES)]
        result = [held.tile([ROWS, PIECE], F32, name=f"result{p}") for p in range(PIECES)]

        zeros = held.tile([ROWS, 1], F32, name="zeros")
        warm = held.tile([ROWS, 1], F32, name="warm")
        nc.vector.memset(zeros[:], 0.0)
        nc.scalar.activation(warm[:], zeros[:], TANH)

        for p in range(PIECES):
            entries = offsets[:, p * OFFSETS : (p + 1) * OFFSETS]
            nc.vector.tensor_tensor(raised[p][:], floors[:].indirect(entries), stream[p][:], MAX)
            nc.scalar.activation(gate[p][:], gates[:].indirect(entries), TANH)
        for p in range(PIECES):
            nc.vector.tensor_tensor(result[p][:], raised[p][:], gate[p][:], MULT)
            nc.sync.dma_start(out[:, p * PIECE : (p + 1) * PIECE], result[p][:])
